import numpy as np
import ml_dtypes


def mxq(x, axis, fmt="e4m3"):
    dtype, down = {"e4m3": (ml_dtypes.float8_e4m3fn, 7), "e5m2": (ml_dtypes.float8_e5m2, 14)}[fmt]
    v = np.moveaxis(np.asarray(x, np.float32).astype(ml_dtypes.bfloat16).astype(np.float64), axis, -1)
    blocks = v.reshape(v.shape[:-1] + (-1, 32))
    amax = np.abs(blocks).max(-1, keepdims=True)
    byte = np.maximum(np.where(amax > 0, np.frexp(amax)[1] - 1 + 127, 0) - down, 1)
    scale = np.exp2(byte - 127.0)
    codes = (blocks / scale).astype(np.float32).astype(dtype).astype(np.float64)
    return np.moveaxis((codes * scale).reshape(v.shape), -1, axis)


WIDE = False


def mx_kscale(k):
    if not WIDE:
        return np.ones(k)
    levels = np.array([10, -10, 5, -5, 0])
    if k % 512:
        return np.exp2(np.random.permutation(np.resize(levels, k // 32))).repeat(32)
    a = np.empty((k // 512, 16))
    for p in range(k // 512):
        a[p, :8] = np.random.permutation(np.resize(levels, 8))
        for g in range(8):
            far = levels[np.abs(levels - a[p, g]) >= 10]
            a[p, g + 8] = far[np.random.randint(len(far))]
    return np.exp2(a.ravel()).repeat(32)


def f64(x):
    return np.asarray(x).astype(np.float64)


def striped(idx):
    return np.tile(idx.reshape(-1, 16).T, (8, 1)).astype(np.uint16)


def unstriped(offs):
    return offs[:16].T.reshape(-1).astype(np.int64)


E2M1 = np.array([0.0, 0.5, 1.0, 1.5, 2.0, 3.0, 4.0, 6.0, -0.0, -0.5, -1.0, -1.5, -2.0, -3.0, -4.0, -6.0])


def pack_weight(w, fmt):
    k, n = w.shape
    w = f64(np.asarray(w, np.float32).astype(ml_dtypes.bfloat16)).reshape(k // 32, 32, n)
    amax = np.abs(w).max(1)
    if fmt == "e4m3":
        byte = np.frexp(amax)[1] - 1 + 127 - 7
    else:
        mant, ex = np.frexp(amax / 6.0)
        byte = np.where(mant > 0.5, ex, ex - 1) + 127
    byte = np.clip(np.where(amax > 0, byte, 1), 1, 254)
    scaled = (w * np.exp2(127.0 - byte)[:, None, :]).reshape(k, n).astype(np.float32)
    by_word = np.ascontiguousarray(scaled.reshape(k // 512, 128, 4, n).transpose(0, 1, 3, 2))
    if fmt == "e4m3":
        words = by_word.astype(ml_dtypes.float8_e4m3fn).view(np.uint8)
    else:
        c = by_word.astype(ml_dtypes.float4_e2m1fn).view(np.uint8) & 0xF
        words = (c[..., 0::2] | (c[..., 1::2] << 4)).reshape(k // 512, 128, 2 * n)
    return np.ascontiguousarray(words), np.ascontiguousarray(byte.astype(np.uint8).reshape(k // 512, 16, n))


def unpack_weight(words, scales, fmt):
    g, _, n = scales.shape
    words = np.ascontiguousarray(words).reshape(g, 128, n, -1)
    if fmt == "e4m3":
        vals = words.view(ml_dtypes.float8_e4m3fn).astype(np.float64)
    else:
        nib = np.empty((g, 128, n, 4), np.uint8)
        nib[..., 0::2] = words & 0xF
        nib[..., 1::2] = words >> 4
        vals = E2M1[nib]
    vals = vals * np.repeat(np.exp2(scales.astype(np.float64) - 127.0), 8, axis=1)[..., None]
    return vals.transpose(0, 1, 3, 2).reshape(g * 512, n)


def gelu(v):
    return 0.5 * v * (1.0 + np.tanh(np.sqrt(2.0 / np.pi) * (v + 0.044715 * v**3)))


def striped8(idx):
    return np.concatenate([v.reshape(-1, 16).T for v in idx]).astype(np.uint16)


def unstriped8(offs):
    return np.stack([offs[16 * g:16 * g + 16].T.reshape(-1) for g in range(8)]).astype(np.int64)


def heads(h, wgt, idx8):
    r = np.arange(h.shape[0])
    return wgt[r // 4 % 128] * h[r[:, None], idx8[r % 512 // 64]]


K, H, N, T, S, P = 1024, 1024, 768, 4096, 1024, 512

def setup_inputs():
    n = np.random.standard_normal
    s = mx_kscale(K)[:, None]
    u = mx_kscale(H)[:, None]
    tab_words, tab_scales = pack_weight(n((K, T)) * s, "e4m3")
    w1_words, w1_scales = pack_weight(n((K, H)) / np.sqrt(K) / s * u.T, "e2m1")
    return {
        "tab_words": tab_words, "tab_scales": tab_scales,
        "w1_words": w1_words, "w1_scales": w1_scales,
        "w2": (0.42 * n((K, H)) / np.sqrt(K) / s).astype(np.float32),
        "b2": np.random.uniform(-0.7, 0.7, H).astype(np.float32),
        "w3": (n((H, N)) / np.sqrt(H) / u).astype(np.float32),
        "wga": np.repeat(np.random.uniform(0.5, 2.0, (8, P)), 16, axis=0).astype(np.float32),
        "wgb": np.repeat(np.random.uniform(0.5, 2.0, (8, P)), 16, axis=0).astype(np.float32),
        "land": np.exp(0.4 * n((N, P))).astype(np.float32),
        "offs": striped(np.random.permutation(T)[:S]),
        "offs2": striped8(np.stack([np.random.permutation(S)[:P] for _ in range(8)])),
        "offs3": striped8(np.stack([np.random.permutation(S)[:P] for _ in range(8)])),
    }

def reference(tab_words, tab_scales, w1_words, w1_scales, w2, b2, w3, wga, wgb, land, offs, offs2, offs3):
    v = unpack_weight(tab_words, tab_scales, "e4m3")[:, unstriped(offs)]
    w1 = unpack_weight(w1_words, w1_scales, "e2m1")
    length = w1.T @ v
    angle = (mxq(f64(w2), 0, "e4m3").T @ v) + f64(b2)[:, None]
    h = length * np.cos(angle)
    xa = heads(h, f64(wga), unstriped8(offs2))
    xb = heads(h, f64(wgb), unstriped8(offs3))
    z = xa + xb
    y = mxq(f64(w3), 0, "e4m3").T @ mxq(z, 0, "e4m3")
    return y * f64(land)

@@ -1,0 +1,275 @@
+import math
+from contextlib import ExitStack
+
+import concourse.mybir as mybir
+
+K, H, N, T, S, M = 1024, 1024, 768, 4096, 1024, 512
+FLOPS = 2 * (2 * K * H * S + H * N * M)
+
+F32 = mybir.dt.float32
+BF16 = mybir.dt.bfloat16
+I32 = mybir.dt.int32
+U32 = mybir.dt.uint32
+U16 = mybir.dt.uint16
+U8 = mybir.dt.uint8
+FP8X4 = mybir.dt.float8_e4m3fn_x4
+FP4X4 = mybir.dt.float4_e2m1fn_x4
+ALU = mybir.AluOpType
+ACT = mybir.ActivationFunctionType
+
+P = 128
+PACK = 4
+PASS = P * PACK
+BANK = 512
+PASSES = K // PASS
+BLOCKS = H // PASS
+N_TILES = N // P
+W3_PIECE = N // 2
+LIST_COLS = 16
+M_CHUNKS = ((0, 256), (256, 512))
+
+
+def tile_list_waggle_patch_scores_kernel(
+    tc, tab_words, tab_scales, w1_words, w1_scales, w2, b2, w3, wga, wgb, land, offs, offs2, offs3, out
+):
+    nc = tc.nc
+    with ExitStack() as ctx:
+        keep = ctx.enter_context(tc.tile_pool(name="keep", bufs=1))
+        ring = ctx.enter_context(tc.tile_pool(name="ring", bufs=2))
+        psum = ctx.enter_context(tc.psum_pool(name="psum", bufs=4))
+
+        idx = keep.tile([P, S // LIST_COLS], U16, name="idx")
+        idx_a = keep.tile([P, M // LIST_COLS], U16, name="idx_a")
+        idx_b = keep.tile([P, M // LIST_COLS], U16, name="idx_b")
+        bias = keep.tile([P, BLOCKS, PACK], F32, name="bias")
+        half_pi = keep.tile([P, 1], F32, name="half_pi")
+        one = keep.tile([P, 1], F32, name="one")
+        tab_w = [keep.tile([P, T], I32, name="tab_w%d" % a) for a in range(PASSES)]
+        tab_s = keep.tile([P, T], U8, name="tab_s")
+        picked_s = keep.tile([P, S], U8, name="picked_s")
+        w1_raw = keep.tile([P, PASSES * H // 2], I32, name="w1_raw")
+        w1_raw_s = keep.tile([P, H], U8, name="w1_raw_s")
+        w1_dealt_s = keep.tile([P, H], U8, name="w1_dealt_s")
+        w1_w = keep.tile([P, PASSES * H], U16, name="w1_w", align_bytes=64)
+        w1_s = keep.tile([P, PASSES * H], U8, name="w1_s", align_bytes=64)
+        v_w = [keep.tile([P, S], U32, name="v_w%d" % a, align_bytes=64) for a in range(PASSES)]
+        v_planes = keep.tile([P, PASSES * S], U8, name="v_planes", align_bytes=64)
+        v_s = [v_planes[:, a * S : (a + 1) * S] for a in range(PASSES)]
+        w2_w = [[keep.tile([P, PASS], U32, name="w2_w%d%d" % (b, a), align_bytes=64) for a in range(PASSES)] for b in range(BLOCKS)]
+        w2_s = [[keep.tile([P, PASS], U8, name="w2_s%d%d" % (b, a), align_bytes=64) for a in range(PASSES)] for b in range(BLOCKS)]
+        w3_w = [[keep.tile([P, W3_PIECE], U32, name="w3_w%d%d" % (b, c), align_bytes=64) for c in range(2)] for b in range(BLOCKS)]
+        w3_s = [[keep.tile([P, W3_PIECE], U8, name="w3_s%d%d" % (b, c), align_bytes=64) for c in range(2)] for b in range(BLOCKS)]
+        wa = keep.tile([P, M], F32, name="wa")
+        wb = keep.tile([P, M], F32, name="wb")
+        z_planes = [keep.tile([P, PACK, M], BF16, name="z_planes%d" % b) for b in range(BLOCKS)]
+        z_w = [keep.tile([P, M], U32, name="z_w%d" % b, align_bytes=64) for b in range(BLOCKS)]
+        z_s = [keep.tile([P, M], U8, name="z_s%d" % b, align_bytes=64) for b in range(BLOCKS)]
+
+        nc.vector.memset(tab_s[0:96, :].bitcast(I32), 0)
+        nc.vector.memset(w1_raw_s[0:96, :].bitcast(I32), 0)
+        nc.gpsimd.memset(w1_s[:].bitcast(I32), 0)
+        nc.gpsimd.memset(v_planes[:].bitcast(I32), 0)
+        nc.gpsimd.memset(one[:], 1.0)
+        nc.gpsimd.tensor_scalar(half_pi[:], one[:], math.pi / 2, 0.0, ALU.mult, ALU.add)
+
+        def load_scale_rows(rows, scales):
+            nc.sync.dma_start(rows[96:P, :].bitcast(I32), scales.bitcast(I32).rearrange("a q t -> q a t"))
+
+        def move_scale_rows(planes, rows):
+            for q in range(4):
+                nc.gpsimd.dma_start(
+                    planes[32 * q : 32 * q + 4, :].bitcast(I32).rearrange("p (a t) -> p a t", a=PASSES),
+                    rows[96 + 8 * q : 96 + 8 * q + 8, :].bitcast(I32),
+                )
+
+        def load_table_words(a):
+            nc.sync.dma_start(tab_w[a][:], tab_words[a].rearrange("p t i -> p (t i)").bitcast(I32))
+
+        def load_rows(w, a, cols):
+            raw = ring.tile([P, PACK, cols.stop - cols.start], F32, name="raw", bufs=4)
+            nc.sync.dma_start(raw[:], w[a * PASS : (a + 1) * PASS, cols].rearrange("(p j) c -> p j c", j=PACK))
+            return raw
+
+        def grouped_tile(columns):
+            return ring.tile([P, columns * PACK], BF16, name="grouped", bufs=3, align_bytes=64)
+
+        def steps(src, dst, grouped, words, scales):
+            half = src.shape[1] // 2
+
+            def first():
+                nc.scalar.copy(dst[:, 0:half], src[:, 0:half])
+
+            def second():
+                nc.scalar.copy(dst[:, half : 2 * half], src[:, half : 2 * half])
+                nc.vector.quantize_mx(out=words.bitcast(FP8X4), scales=scales, in_=grouped[:])
+
+            return [first, second]
+
+        def w2_steps(raw, b, a):
+            grouped = grouped_tile(PASS)
+            dst = grouped[:].rearrange("p (i q j) -> p q j i", i=PACK, j=PACK)
+            src = raw[:].rearrange("p j (q i) -> p q j i", i=PACK)
+            return steps(src, dst, grouped, w2_w[b][a][:], w2_s[b][a][:])
+
+        def w3_steps(raw, b, c):
+            grouped = grouped_tile(W3_PIECE)
+            dst = grouped[:].rearrange("p (c i j) -> p c j i", i=4, j=PACK)
+            src = raw[:].rearrange("p j (c i) -> p c j i", i=4)
+            return steps(src, dst, grouped, w3_w[b][c][:], w3_s[b][c][:])
+
+        def z_steps(b, m0, m1):
+            grouped = grouped_tile(m1 - m0)
+            dst = grouped[:].rearrange("p (c i j) -> p c j i", i=4, j=PACK)
+            src = z_planes[b][:, :, m0:m1].rearrange("p j (c i) -> p c j i", i=4)
+            return steps(src, dst, grouped, z_w[b][:, m0:m1], z_s[b][:, m0:m1])
+
+        nc.sync.dma_start(idx[:], offs)
+        load_scale_rows(tab_s, tab_scales)
+        load_scale_rows(w1_raw_s, w1_scales)
+        nc.sync.dma_start(
+            w1_raw[:].rearrange("p (a c) -> p a c", a=PASSES), w1_words.bitcast(I32).rearrange("a p c -> p a c")
+        )
+        load_table_words(0)
+        w2_raw = [load_rows(w2, a, slice(0, PASS)) for a in range(PASSES)]
+        load_table_words(1)
+        nc.sync.dma_start(bias[:], b2.rearrange("(b p i) -> p b i", p=P, i=PACK))
+        nc.sync.dma_start(idx_a[:], offs2)
+        nc.sync.dma_start(idx_b[:], offs3)
+        nc.sync.dma_start(wa[:], wga)
+        nc.sync.dma_start(wb[:], wgb)
+
+        nc.vector.tensor_copy(
+            w1_dealt_s[:].rearrange("p (g i q) -> p g i q", i=PACK, q=P),
+            w1_raw_s[:].rearrange("p (g q i) -> p g i q", i=PACK, q=P),
+        )
+        move_scale_rows(w1_s, w1_dealt_s)
+        nc.vector.tensor_copy(picked_s[:], tab_s[:].indirect(idx[:]))
+        move_scale_rows(v_planes, picked_s)
+        nc.vector.tensor_copy(
+            w1_w[:].rearrange("p (g i q) -> p g i q", i=PACK, q=P),
+            w1_raw[:].bitcast(U16).rearrange("p (g q i) -> p g i q", i=PACK, q=P),
+        )
+        nc.vector.tensor_copy(v_w[0][:], tab_w[0][:].bitcast(U32).indirect(idx[:]))
+        for a in range(PASSES):
+            for step in w2_steps(w2_raw[a], 0, a):
+                step()
+        for c in range(2):
+            nc.vector.tensor_copy(
+                v_w[1][:, c * BANK : (c + 1) * BANK],
+                tab_w[1][:].bitcast(U32).indirect(idx[:, c * BANK // LIST_COLS : (c + 1) * BANK // LIST_COLS]),
+            )
+
+        w2_late = [load_rows(w2, a, slice(PASS, 2 * PASS)) for a in range(PASSES)]
+        w3_raw = [[load_rows(w3, b, slice(c * W3_PIECE, (c + 1) * W3_PIECE)) for c in range(2)] for b in range(BLOCKS)]
+        land_t = keep.tile([P, N_TILES, M], F32, name="tab_w1")
+        nc.sync.dma_start(land_t[:], land.rearrange("(t p) m -> p t m", p=P))
+
+        def make_h(b, i):
+            halves = [slice(c * BANK, (c + 1) * BANK) for c in range(2)]
+            angle = [psum.tile([P, BANK], F32, name="angle") for c in range(2)]
+            length = [psum.tile([P, BANK], F32, name="length") for c in range(2)]
+            for c in range(2):
+                for a in range(PASSES):
+                    nc.tensor.matmul_mx(
+                        out=angle[c][:],
+                        lhsT=w2_w[b][a][:, i * P : (i + 1) * P].bitcast(FP8X4),
+                        lhsT_scale=w2_s[b][a][:, i * P : (i + 1) * P],
+                        rhs=v_w[a][:, halves[c]].bitcast(FP8X4),
+                        rhs_scale=v_s[a][:, halves[c]],
+                        start=(a == 0),
+                        stop=(a == PASSES - 1),
+                    )
+            for c in range(2):
+                for a in range(PASSES):
+                    col = a * H + b * PASS + i * P
+                    nc.tensor.matmul_mx(
+                        out=length[c][:],
+                        lhsT=w1_w[:, col : col + P].bitcast(FP4X4),
+                        lhsT_scale=w1_s[:, col : col + P],
+                        rhs=v_w[a][:, halves[c]].bitcast(FP8X4),
+                        rhs_scale=v_s[a][:, halves[c]],
+                        start=(a == 0),
+                        stop=(a == PASSES - 1),
+                    )
+            size = [ring.tile([P, BANK], F32, name="size", bufs=3) for c in range(2)]
+            cosine = [ring.tile([P, BANK], F32, name="cosine", bufs=4) for c in range(2)]
+            for c in range(2):
+                nc.scalar.activation(size[c][:], angle[c][:], ACT.Abs, bias=bias[:, b, i : i + 1])
+            for c in range(2):
+                nc.scalar.activation(cosine[c][:], size[c][:], ACT.Sin, bias=half_pi[:], scale=-1.0)
+            h = ring.tile([P, S], F32, name="h", bufs=3)
+            for c in range(2):
+                nc.vector.tensor_tensor(h[:, halves[c]], length[c][:], cosine[c][:], ALU.mult)
+            return h
+
+        def pick(h, b, i, m0, m1, tag="x", bufs=3):
+            cols = slice(m0 // LIST_COLS, m1 // LIST_COLS)
+            xa = ring.tile([P, m1 - m0], F32, name=tag + "a", bufs=bufs)
+            xb = ring.tile([P, m1 - m0], F32, name=tag + "b", bufs=bufs)
+            nc.vector.tensor_tensor(xa[:], h[:].indirect(idx_a[:, cols]), wa[:, m0:m1], ALU.mult)
+            nc.vector.tensor_tensor(xb[:], h[:].indirect(idx_b[:, cols]), wb[:, m0:m1], ALU.mult)
+            nc.gpsimd.tensor_tensor(z_planes[b][:, i, m0:m1], xa[:], xb[:], ALU.add)
+
+        def score_passes(y, b, n0, m0, m1):
+            per_bank = BANK // (m1 - m0)
+            for u in range(per_bank):
+                c, col = divmod((n0 + u) * P, W3_PIECE)
+                nc.tensor.matmul_mx(
+                    out=y[:, u, :],
+                    lhsT=w3_w[b][c][:, col : col + P].bitcast(FP8X4),
+                    lhsT_scale=w3_s[b][c][:, col : col + P],
+                    rhs=z_w[b][:, m0:m1].bitcast(FP8X4),
+                    rhs_scale=z_s[b][:, m0:m1],
+                    start=(b == 0 and u == 0),
+                    stop=(b == BLOCKS - 1 and u == per_bank - 1),
+                )
+
+        def weigh_and_store(y, n0, m0, m1):
+            per_bank = BANK // (m1 - m0)
+            result = ring.tile([P, per_bank, m1 - m0], F32, name="result", bufs=6)
+            nc.vector.tensor_tensor(result[:], y[:], land_t[:, n0 : n0 + per_bank, m0:m1], ALU.mult)
+            nc.sync.dma_start(out[n0 * P : (n0 + per_bank) * P, m0:m1].rearrange("(t p) m -> p t m", p=P), result[:])
+
+        side_makers = [
+            lambda: w2_steps(w2_late[0], 1, 0),
+            lambda: w2_steps(w2_late[1], 1, 1),
+            lambda: w3_steps(w3_raw[0][0], 0, 0),
+            lambda: w3_steps(w3_raw[0][1], 0, 1),
+            lambda: z_steps(0, 0, M),
+            lambda: w3_steps(w3_raw[1][0], 1, 0),
+            lambda: w3_steps(w3_raw[1][1], 1, 1),
+        ]
+        side_counts = (1, 2, 1, 2, 2, 1, 2, 3)
+        pending = []
+        made = 0
+        tiles = [(b, i) for b in range(BLOCKS) for i in range(PACK)]
+        for t, (b, i) in enumerate(tiles):
+            h = make_h(b, i)
+            if t < len(tiles) - 2:
+                pick(h, b, i, 0, M)
+            elif t == len(tiles) - 2:
+                pick(h, b, i, *M_CHUNKS[0])
+                h_before = h
+            else:
+                pick(h, b, i, *M_CHUNKS[0], tag="late", bufs=1)
+                pick(h, b, i, *M_CHUNKS[1])
+                pick(h_before, b, i - 1, *M_CHUNKS[1], tag="late", bufs=1)
+            for u in range(side_counts[t]):
+                if not pending:
+                    pending = side_makers[made]()
+                    made = made + 1
+                pending[0]()
+                pending = pending[1:]
+
+        banks = []
+        for m0, m1 in M_CHUNKS:
+            for n0 in range(0, N_TILES, BANK // (m1 - m0)):
+                y = psum.tile([P, BANK // (m1 - m0), m1 - m0], F32, name="angle" if len(banks) < 4 else "length")
+                banks.append((y, n0, m0, m1))
+                score_passes(y, 0, n0, m0, m1)
+        for m0, m1 in M_CHUNKS:
+            for step in z_steps(1, m0, m1):
+                step()
+        for y, n0, m0, m1 in banks:
+            score_passes(y, 1, n0, m0, m1)
+            weigh_and_store(y, n0, m0, m1)

@@ -44,7 +44,7 @@ def tile_list_waggle_patch_scores_kernel(
         bias = keep.tile([P, BLOCKS, PACK], F32, name="bias")
         half_pi = keep.tile([P, 1], F32, name="half_pi")
         one = keep.tile([P, 1], F32, name="one")
-        tab_w = [keep.tile([P, T], I32, name="tab_w%d" % a) for a in range(PASSES)]
+        warm = keep.tile([P, 1], F32, name="warm")
         tab_s = keep.tile([P, T], U8, name="tab_s")
         picked_s = keep.tile([P, S], U8, name="picked_s")
         w1_raw = keep.tile([P, PASSES * H // 2], I32, name="w1_raw")
@@ -59,9 +59,9 @@ def tile_list_waggle_patch_scores_kernel(
         w2_s = [[keep.tile([P, PASS], U8, name="w2_s%d%d" % (b, a), align_bytes=64) for a in range(PASSES)] for b in range(BLOCKS)]
         w3_w = [[keep.tile([P, W3_PIECE], U32, name="w3_w%d%d" % (b, c), align_bytes=64) for c in range(2)] for b in range(BLOCKS)]
         w3_s = [[keep.tile([P, W3_PIECE], U8, name="w3_s%d%d" % (b, c), align_bytes=64) for c in range(2)] for b in range(BLOCKS)]
-        wa = keep.tile([P, M], F32, name="wa")
-        wb = keep.tile([P, M], F32, name="wb")
-        z_planes = [keep.tile([P, PACK, M], BF16, name="z_planes%d" % b) for b in range(BLOCKS)]
+        z_planes = {(0, 0): keep.tile([P, PACK, M], BF16, name="z_planes0")}
+        for m0, m1 in M_CHUNKS:
+            z_planes[(1, m0)] = keep.tile([P, PACK, m1 - m0], BF16, name="z_planes1_%d" % m0)
         z_w = [keep.tile([P, M], U32, name="z_w%d" % b, align_bytes=64) for b in range(BLOCKS)]
         z_s = [keep.tile([P, M], U8, name="z_s%d" % b, align_bytes=64) for b in range(BLOCKS)]
 
@@ -71,22 +71,25 @@ def tile_list_waggle_patch_scores_kernel(
         nc.gpsimd.memset(v_planes[:].bitcast(I32), 0)
         nc.gpsimd.memset(one[:], 1.0)
         nc.gpsimd.tensor_scalar(half_pi[:], one[:], math.pi / 2, 0.0, ALU.mult, ALU.add)
+        nc.scalar.activation(warm[:], one[:], ACT.Sin)
 
         def load_scale_rows(rows, scales):
             nc.sync.dma_start(rows[96:P, :].bitcast(I32), scales.bitcast(I32).rearrange("a q t -> q a t"))
 
-        def move_scale_rows(planes, rows):
+        def move_scale_rows(queue, planes, rows):
             for q in range(4):
-                nc.gpsimd.dma_start(
+                queue.dma_start(
                     planes[32 * q : 32 * q + 4, :].bitcast(I32).rearrange("p (a t) -> p a t", a=PASSES),
                     rows[96 + 8 * q : 96 + 8 * q + 8, :].bitcast(I32),
                 )
 
-        def load_table_words(a):
-            nc.sync.dma_start(tab_w[a][:], tab_words[a].rearrange("p t i -> p (t i)").bitcast(I32))
+        def load_table_words(a, slot):
+            words = keep.tile([P, T], I32, name=slot)
+            nc.sync.dma_start(words[:], tab_words[a].rearrange("p t i -> p (t i)").bitcast(I32))
+            return words
 
-        def load_rows(w, a, cols):
-            raw = ring.tile([P, PACK, cols.stop - cols.start], F32, name="raw", bufs=4)
+        def load_rows(w, a, cols, slot):
+            raw = keep.tile([P, PACK, cols.stop - cols.start], F32, name=slot)
             nc.sync.dma_start(raw[:], w[a * PASS : (a + 1) * PASS, cols].rearrange("(p j) c -> p j c", j=PACK))
             return raw
 
@@ -120,49 +123,59 @@ def tile_list_waggle_patch_scores_kernel(
         def z_steps(b, m0, m1):
             grouped = grouped_tile(m1 - m0)
             dst = grouped[:].rearrange("p (c i j) -> p c j i", i=4, j=PACK)
-            src = z_planes[b][:, :, m0:m1].rearrange("p j (c i) -> p c j i", i=4)
+            src = z_planes[(b, m0)][:].rearrange("p j (c i) -> p c j i", i=4)
             return steps(src, dst, grouped, z_w[b][:, m0:m1], z_s[b][:, m0:m1])
 
         nc.sync.dma_start(idx[:], offs)
-        load_scale_rows(tab_s, tab_scales)
+        nc.sync.dma_start(idx_a[:], offs2)
+        nc.sync.dma_start(idx_b[:], offs3)
+        nc.gpsimd.dma_start(bias[:], b2.rearrange("(b p i) -> p b i", p=P, i=PACK))
         load_scale_rows(w1_raw_s, w1_scales)
+        load_scale_rows(tab_s, tab_scales)
         nc.sync.dma_start(
             w1_raw[:].rearrange("p (a c) -> p a c", a=PASSES), w1_words.bitcast(I32).rearrange("a p c -> p a c")
         )
-        load_table_words(0)
-        w2_raw = [load_rows(w2, a, slice(0, PASS)) for a in range(PASSES)]
-        load_table_words(1)
-        nc.sync.dma_start(bias[:], b2.rearrange("(b p i) -> p b i", p=P, i=PACK))
-        nc.sync.dma_start(idx_a[:], offs2)
-        nc.sync.dma_start(idx_b[:], offs3)
-        nc.sync.dma_start(wa[:], wga)
-        nc.sync.dma_start(wb[:], wgb)
+        tab_first = load_table_words(0, "slot_b")
+        w2_first = load_rows(w2, 0, slice(0, PASS), "slot_a")
+        tab_second = load_table_words(1, "slot_c")
 
         nc.vector.tensor_copy(
             w1_dealt_s[:].rearrange("p (g i q) -> p g i q", i=PACK, q=P),
             w1_raw_s[:].rearrange("p (g q i) -> p g i q", i=PACK, q=P),
         )
-        move_scale_rows(w1_s, w1_dealt_s)
+        move_scale_rows(nc.gpsimd, w1_s, w1_dealt_s)
         nc.vector.tensor_copy(picked_s[:], tab_s[:].indirect(idx[:]))
-        move_scale_rows(v_planes, picked_s)
+        move_scale_rows(nc.scalar, v_planes, picked_s)
         nc.vector.tensor_copy(
             w1_w[:].rearrange("p (g i q) -> p g i q", i=PACK, q=P),
             w1_raw[:].bitcast(U16).rearrange("p (g q i) -> p g i q", i=PACK, q=P),
         )
-        nc.vector.tensor_copy(v_w[0][:], tab_w[0][:].bitcast(U32).indirect(idx[:]))
-        for a in range(PASSES):
-            for step in w2_steps(w2_raw[a], 0, a):
-                step()
+        nc.vector.tensor_copy(v_w[0][:], tab_first[:].bitcast(U32).indirect(idx[:]))
+        w2_second = load_rows(w2, 1, slice(0, PASS), "slot_b")
+        weights = keep.tile([P, 2, M], F32, name="picked_s")
+        wa = weights[:, 0, :]
+        wb = weights[:, 1, :]
+        nc.sync.dma_start(wa, wga)
+        nc.sync.dma_start(wb, wgb)
+        for step in w2_steps(w2_first, 0, 0):
+            step()
         for c in range(2):
             nc.vector.tensor_copy(
                 v_w[1][:, c * BANK : (c + 1) * BANK],
-                tab_w[1][:].bitcast(U32).indirect(idx[:, c * BANK // LIST_COLS : (c + 1) * BANK // LIST_COLS]),
+                tab_second[:].bitcast(U32).indirect(idx[:, c * BANK // LIST_COLS : (c + 1) * BANK // LIST_COLS]),
+            )
+        by_plane = w2_second[:].rearrange("p j (q i) -> p q j i", i=PACK)
+        for i0, i1 in ((0, 1), (1, PACK)):
+            grouped = grouped_tile((i1 - i0) * P)
+            nc.vector.tensor_copy(grouped[:].rearrange("p (i q j) -> p q j i", q=P, j=PACK), by_plane[:, :, :, i0:i1])
+            nc.vector.quantize_mx(
+                out=w2_w[0][1][:, i0 * P : i1 * P].bitcast(FP8X4), scales=w2_s[0][1][:, i0 * P : i1 * P], in_=grouped[:]
             )
 
-        w2_late = [load_rows(w2, a, slice(PASS, 2 * PASS)) for a in range(PASSES)]
-        w3_raw = [[load_rows(w3, b, slice(c * W3_PIECE, (c + 1) * W3_PIECE)) for c in range(2)] for b in range(BLOCKS)]
-        land_t = keep.tile([P, N_TILES, M], F32, name="tab_w1")
-        nc.sync.dma_start(land_t[:], land.rearrange("(t p) m -> p t m", p=P))
+        w2_late = [load_rows(w2, a, slice(PASS, 2 * PASS), ("slot_a", "slot_c")[a]) for a in range(PASSES)]
+
+        def load_w3(b, c):
+            return load_rows(w3, b, slice(c * W3_PIECE, (c + 1) * W3_PIECE), ("slot_b", "slot_a")[c])
 
         def make_h(b, i):
             halves = [slice(c * BANK, (c + 1) * BANK) for c in range(2)]
@@ -202,13 +215,22 @@ def tile_list_waggle_patch_scores_kernel(
                 nc.vector.tensor_tensor(h[:, halves[c]], length[c][:], cosine[c][:], ALU.mult)
             return h
 
-        def pick(h, b, i, m0, m1, tag="x", bufs=3):
+        def pick(h, b, i, m0, m1, held=None):
             cols = slice(m0 // LIST_COLS, m1 // LIST_COLS)
-            xa = ring.tile([P, m1 - m0], F32, name=tag + "a", bufs=bufs)
-            xb = ring.tile([P, m1 - m0], F32, name=tag + "b", bufs=bufs)
+            if held is None:
+                xa = ring.tile([P, m1 - m0], F32, name="xa", bufs=3)
+                xb = ring.tile([P, m1 - m0], F32, name="xb", bufs=3)
+            else:
+                pair = keep.tile([P, 2, m1 - m0], F32, name=held)
+                xa, xb = pair[:, 0, :], pair[:, 1, :]
             nc.vector.tensor_tensor(xa[:], h[:].indirect(idx_a[:, cols]), wa[:, m0:m1], ALU.mult)
             nc.vector.tensor_tensor(xb[:], h[:].indirect(idx_b[:, cols]), wb[:, m0:m1], ALU.mult)
-            nc.gpsimd.tensor_tensor(z_planes[b][:, i, m0:m1], xa[:], xb[:], ALU.add)
+            for c0, c1 in ((0, M),) if b == 0 else M_CHUNKS:
+                lo, hi = max(c0, m0), min(c1, m1)
+                if lo < hi:
+                    nc.gpsimd.tensor_tensor(
+                        z_planes[(b, c0)][:, i, lo - c0 : hi - c0], xa[:, lo - m0 : hi - m0], xb[:, lo - m0 : hi - m0], ALU.add
+                    )
 
         def score_passes(y, b, n0, m0, m1):
             per_bank = BANK // (m1 - m0)
@@ -224,12 +246,14 @@ def tile_list_waggle_patch_scores_kernel(
                     stop=(b == BLOCKS - 1 and u == per_bank - 1),
                 )
 
-        def weigh_and_store(y, n0, m0, m1):
-            per_bank = BANK // (m1 - m0)
-            result = ring.tile([P, per_bank, m1 - m0], F32, name="result", bufs=6)
-            nc.vector.tensor_tensor(result[:], y[:], land_t[:, n0 : n0 + per_bank, m0:m1], ALU.mult)
-            nc.sync.dma_start(out[n0 * P : (n0 + per_bank) * P, m0:m1].rearrange("(t p) m -> p t m", p=P), result[:])
+        def weigh_and_store(y, n0, m0, m1, u0, u1, queue):
+            result = ring.tile([P, u1 - u0, m1 - m0], F32, name="result", bufs=7)
+            nc.vector.tensor_tensor(result[:], y[:, u0:u1, :], land_t[:, n0 + u0 : n0 + u1, m0:m1], ALU.mult)
+            queue.dma_start(out[(n0 + u0) * P : (n0 + u1) * P, m0:m1].rearrange("(t p) m -> p t m", p=P), result[:])
 
+        w3_raw = [[load_w3(b, c) for c in range(2)] for b in range(BLOCKS)]
+        land_t = keep.tile([P, N_TILES, M], F32, name="slot_c")
+        nc.sync.dma_start(land_t[:], land.rearrange("(t p) m -> p t m", p=P))
         side_makers = [
             lambda: w2_steps(w2_late[0], 1, 0),
             lambda: w2_steps(w2_late[1], 1, 1),
@@ -251,9 +275,9 @@ def tile_list_waggle_patch_scores_kernel(
                 pick(h, b, i, *M_CHUNKS[0])
                 h_before = h
             else:
-                pick(h, b, i, *M_CHUNKS[0], tag="late", bufs=1)
+                pick(h, b, i, *M_CHUNKS[0], held="late")
                 pick(h, b, i, *M_CHUNKS[1])
-                pick(h_before, b, i - 1, *M_CHUNKS[1], tag="late", bufs=1)
+                pick(h_before, b, i - 1, 256, 384, held="late")
             for u in range(side_counts[t]):
                 if not pending:
                     pending = side_makers[made]()
@@ -267,9 +291,15 @@ def tile_list_waggle_patch_scores_kernel(
                 y = psum.tile([P, BANK // (m1 - m0), m1 - m0], F32, name="angle" if len(banks) < 4 else "length")
                 banks.append((y, n0, m0, m1))
                 score_passes(y, 0, n0, m0, m1)
-        for m0, m1 in M_CHUNKS:
-            for step in z_steps(1, m0, m1):
-                step()
+        for step in z_steps(1, *M_CHUNKS[0]):
+            step()
+        pick(h_before, 1, PACK - 2, 384, 512, held="z_planes1_0")
+        for step in z_steps(1, *M_CHUNKS[1]):
+            step()
         for y, n0, m0, m1 in banks:
             score_passes(y, 1, n0, m0, m1)
-            weigh_and_store(y, n0, m0, m1)
+            if y is banks[-1][0]:
+                weigh_and_store(y, n0, m0, m1, 0, 1, nc.sync)
+                weigh_and_store(y, n0, m0, m1, 1, 2, nc.scalar)
+            else:
+                weigh_and_store(y, n0, m0, m1, 0, 2, nc.sync)

@@ -36,7 +36,7 @@ def tile_list_waggle_patch_scores_kernel(
     with ExitStack() as ctx:
         keep = ctx.enter_context(tc.tile_pool(name="keep", bufs=1))
         ring = ctx.enter_context(tc.tile_pool(name="ring", bufs=2))
-        psum = ctx.enter_context(tc.psum_pool(name="psum", bufs=4))
+        psum = ctx.enter_context(tc.psum_pool(name="psum", bufs=2))
 
         idx = keep.tile([P, S // LIST_COLS], U16, name="idx")
         idx_a = keep.tile([P, M // LIST_COLS], U16, name="idx_a")
@@ -110,8 +110,8 @@ def tile_list_waggle_patch_scores_kernel(
 
         def w2_steps(raw, b, a):
             grouped = grouped_tile(PASS)
-            dst = grouped[:].rearrange("p (i q j) -> p q j i", i=PACK, j=PACK)
-            src = raw[:].rearrange("p j (q i) -> p q j i", i=PACK)
+            dst = grouped[:].rearrange("p (i q j) -> p q i j", i=PACK, j=PACK)
+            src = raw[:].rearrange("p j (q i) -> p q i j", i=PACK)
             return steps(src, dst, grouped, w2_w[b][a][:], w2_s[b][a][:])
 
         def w3_steps(raw, b, c):
@@ -164,20 +164,22 @@ def tile_list_waggle_patch_scores_kernel(
                 v_w[1][:, c * BANK : (c + 1) * BANK],
                 tab_second[:].bitcast(U32).indirect(idx[:, c * BANK // LIST_COLS : (c + 1) * BANK // LIST_COLS]),
             )
-        by_plane = w2_second[:].rearrange("p j (q i) -> p q j i", i=PACK)
-        for i0, i1 in ((0, 1), (1, PACK)):
-            grouped = grouped_tile((i1 - i0) * P)
-            nc.vector.tensor_copy(grouped[:].rearrange("p (i q j) -> p q j i", q=P, j=PACK), by_plane[:, :, :, i0:i1])
-            nc.vector.quantize_mx(
-                out=w2_w[0][1][:, i0 * P : i1 * P].bitcast(FP8X4), scales=w2_s[0][1][:, i0 * P : i1 * P], in_=grouped[:]
-            )
+        by_plane = w2_second[:].rearrange("p j (q i) -> p i q j", i=PACK)
+        first_plane = grouped_tile(P)
+        nc.vector.tensor_copy(first_plane[:].rearrange("p (q j) -> p q j", j=PACK), by_plane[:, 0])
+        nc.vector.quantize_mx(out=w2_w[0][1][:, 0:P].bitcast(FP8X4), scales=w2_s[0][1][:, 0:P], in_=first_plane[:])
+        other_planes = grouped_tile(PASS - P)
+        others = other_planes[:].rearrange("p (i q j) -> p i q j", q=P, j=PACK)
+        nc.scalar.copy(others[:, 0], by_plane[:, 1])
+        nc.vector.tensor_copy(others[:, 1:3], by_plane[:, 2:4])
+        nc.vector.quantize_mx(out=w2_w[0][1][:, P:PASS].bitcast(FP8X4), scales=w2_s[0][1][:, P:PASS], in_=other_planes[:])
 
         w2_late = [load_rows(w2, a, slice(PASS, 2 * PASS), ("slot_a", "slot_c")[a]) for a in range(PASSES)]
 
         def load_w3(b, c):
             return load_rows(w3, b, slice(c * W3_PIECE, (c + 1) * W3_PIECE), ("slot_b", "slot_a")[c])
 
-        def make_h(b, i):
+        def make_h(b, i, slot):
             halves = [slice(c * BANK, (c + 1) * BANK) for c in range(2)]
             angle = [psum.tile([P, BANK], F32, name="angle") for c in range(2)]
             length = [psum.tile([P, BANK], F32, name="length") for c in range(2)]
@@ -204,7 +206,7 @@ def tile_list_waggle_patch_scores_kernel(
                         start=(a == 0),
                         stop=(a == PASSES - 1),
                     )
-            size = [ring.tile([P, BANK], F32, name="size", bufs=3) for c in range(2)]
+            size = [ring.tile([P, BANK], F32, name="size", bufs=2), keep.tile([P, BANK], F32, name=slot)]
             cosine = [ring.tile([P, BANK], F32, name="cosine", bufs=4) for c in range(2)]
             for c in range(2):
                 nc.scalar.activation(size[c][:], angle[c][:], ACT.Abs, bias=bias[:, b, i : i + 1])
@@ -215,22 +217,11 @@ def tile_list_waggle_patch_scores_kernel(
                 nc.vector.tensor_tensor(h[:, halves[c]], length[c][:], cosine[c][:], ALU.mult)
             return h
 
-        def pick(h, b, i, m0, m1, held=None):
-            cols = slice(m0 // LIST_COLS, m1 // LIST_COLS)
-            if held is None:
-                xa = ring.tile([P, m1 - m0], F32, name="xa", bufs=3)
-                xb = ring.tile([P, m1 - m0], F32, name="xb", bufs=3)
-            else:
-                pair = keep.tile([P, 2, m1 - m0], F32, name=held)
-                xa, xb = pair[:, 0, :], pair[:, 1, :]
-            nc.vector.tensor_tensor(xa[:], h[:].indirect(idx_a[:, cols]), wa[:, m0:m1], ALU.mult)
-            nc.vector.tensor_tensor(xb[:], h[:].indirect(idx_b[:, cols]), wb[:, m0:m1], ALU.mult)
-            for c0, c1 in ((0, M),) if b == 0 else M_CHUNKS:
-                lo, hi = max(c0, m0), min(c1, m1)
-                if lo < hi:
-                    nc.gpsimd.tensor_tensor(
-                        z_planes[(b, c0)][:, i, lo - c0 : hi - c0], xa[:, lo - m0 : hi - m0], xb[:, lo - m0 : hi - m0], ALU.add
-                    )
+        def pick(x, h, lists, weight, m0, m1):
+            nc.vector.tensor_tensor(x, h[:].indirect(lists[:, m0 // LIST_COLS : m1 // LIST_COLS]), weight[:, m0:m1], ALU.mult)
+
+        def z_part(b, i, m0, m1):
+            return z_planes[(0, 0)][:, i, m0:m1] if b == 0 else z_planes[(1, m0)][:, i, :]
 
         def score_passes(y, b, n0, m0, m1):
             per_bank = BANK // (m1 - m0)
@@ -267,17 +258,33 @@ def tile_list_waggle_patch_scores_kernel(
         pending = []
         made = 0
         tiles = [(b, i) for b in range(BLOCKS) for i in range(PACK)]
+        low, high = M_CHUNKS
+        last = len(tiles) - 1
+        before = None
         for t, (b, i) in enumerate(tiles):
-            h = make_h(b, i)
-            if t < len(tiles) - 2:
-                pick(h, b, i, 0, M)
-            elif t == len(tiles) - 2:
-                pick(h, b, i, *M_CHUNKS[0])
-                h_before = h
+            slot = "size_high%d" % (t % 2)
+            h = make_h(b, i, slot)
+            xa = ring.tile([P, M], F32, name="xa", bufs=3)
+            xb_low = ring.tile([P, low[1]], F32, name="xb", bufs=3)
+            if before is not None:
+                xb_high = keep.tile([P, M - low[1]], F32, name=slot)
+                pick(xb_high[:], before[0], idx_b, wb, *high)
+            if t < last:
+                pick(xa[:], h, idx_a, wa, 0, M)
             else:
-                pick(h, b, i, *M_CHUNKS[0], held="late")
-                pick(h, b, i, *M_CHUNKS[1])
-                pick(h_before, b, i - 1, 256, 384, held="late")
+                pick(xa[:, 0 : low[1]], h, idx_a, wa, *low)
+            if before is not None:
+                nc.vector.tensor_tensor(z_part(*tiles[t - 1], *high), before[1][:, low[1] : M], xb_high[:], ALU.add)
+            pick(xb_low[:], h, idx_b, wb, *low)
+            if t < last:
+                nc.gpsimd.tensor_tensor(z_part(b, i, *low), xa[:, 0 : low[1]], xb_low[:], ALU.add)
+            else:
+                xb_high = ring.tile([P, M - low[1]], F32, name="xb", bufs=3)
+                pick(xa[:, low[1] : M], h, idx_a, wa, *high)
+                nc.vector.tensor_tensor(z_part(b, i, *low), xa[:, 0 : low[1]], xb_low[:], ALU.add)
+                pick(xb_high[:], h, idx_b, wb, *high)
+                nc.vector.tensor_tensor(z_part(b, i, *high), xa[:, low[1] : M], xb_high[:], ALU.add)
+            before = (h, xa)
             for u in range(side_counts[t]):
                 if not pending:
                     pending = side_makers[made]()
@@ -288,14 +295,15 @@ def tile_list_waggle_patch_scores_kernel(
         banks = []
         for m0, m1 in M_CHUNKS:
             for n0 in range(0, N_TILES, BANK // (m1 - m0)):
-                y = psum.tile([P, BANK // (m1 - m0), m1 - m0], F32, name="angle" if len(banks) < 4 else "length")
+                if len(banks) < 4:
+                    y = psum.tile([P, BANK // (m1 - m0), m1 - m0], F32, name="scores", bufs=4)
+                else:
+                    y = psum.tile([P, BANK // (m1 - m0), m1 - m0], F32, name="angle")
                 banks.append((y, n0, m0, m1))
                 score_passes(y, 0, n0, m0, m1)
-        for step in z_steps(1, *M_CHUNKS[0]):
-            step()
-        pick(h_before, 1, PACK - 2, 384, 512, held="z_planes1_0")
-        for step in z_steps(1, *M_CHUNKS[1]):
-            step()
+        for m0, m1 in M_CHUNKS:
+            for step in z_steps(1, m0, m1):
+                step()
         for y, n0, m0, m1 in banks:
             score_passes(y, 1, n0, m0, m1)
             if y is banks[-1][0]:

@@ -47,10 +47,9 @@ def tile_list_waggle_patch_scores_kernel(
         warm = keep.tile([P, 1], F32, name="warm")
         tab_s = keep.tile([P, T], U8, name="tab_s")
         picked_s = keep.tile([P, S], U8, name="picked_s")
-        w1_raw = keep.tile([P, PASSES * H // 2], I32, name="w1_raw")
         w1_raw_s = keep.tile([P, H], U8, name="w1_raw_s")
         w1_dealt_s = keep.tile([P, H], U8, name="w1_dealt_s")
-        w1_w = keep.tile([P, PASSES * H], U16, name="w1_w", align_bytes=64)
+        w1_w = [keep.tile([P, PASSES * PASS], U16, name="w1_w%d" % b, align_bytes=64) for b in range(BLOCKS)]
         w1_s = keep.tile([P, PASSES * H], U8, name="w1_s", align_bytes=64)
         v_w = [keep.tile([P, S], U32, name="v_w%d" % a, align_bytes=64) for a in range(PASSES)]
         v_planes = keep.tile([P, PASSES * S], U8, name="v_planes", align_bytes=64)
@@ -59,9 +58,7 @@ def tile_list_waggle_patch_scores_kernel(
         w2_s = [[keep.tile([P, PASS], U8, name="w2_s%d%d" % (b, a), align_bytes=64) for a in range(PASSES)] for b in range(BLOCKS)]
         w3_w = [[keep.tile([P, W3_PIECE], U32, name="w3_w%d%d" % (b, c), align_bytes=64) for c in range(2)] for b in range(BLOCKS)]
         w3_s = [[keep.tile([P, W3_PIECE], U8, name="w3_s%d%d" % (b, c), align_bytes=64) for c in range(2)] for b in range(BLOCKS)]
-        z_planes = {(0, 0): keep.tile([P, PACK, M], BF16, name="z_planes0")}
-        for m0, m1 in M_CHUNKS:
-            z_planes[(1, m0)] = keep.tile([P, PACK, m1 - m0], BF16, name="z_planes1_%d" % m0)
+        z_planes = [keep.tile([P, PACK, M], BF16, name="z_planes%d" % b) for b in range(BLOCKS)]
         z_w = [keep.tile([P, M], U32, name="z_w%d" % b, align_bytes=64) for b in range(BLOCKS)]
         z_s = [keep.tile([P, M], U8, name="z_s%d" % b, align_bytes=64) for b in range(BLOCKS)]
 
@@ -83,6 +80,18 @@ def tile_list_waggle_patch_scores_kernel(
                     rows[96 + 8 * q : 96 + 8 * q + 8, :].bitcast(I32),
                 )
 
+        def load_w1_words(b, slot):
+            raw = keep.tile([P, PASSES, PASS // 2], I32, name=slot)
+            rows = w1_words.bitcast(I32).rearrange("a p c -> p a c")
+            nc.sync.dma_start(raw[:], rows[:, :, b * PASS // 2 : (b + 1) * PASS // 2])
+            return raw
+
+        def deal_w1_words(raw, b):
+            nc.vector.tensor_copy(
+                w1_w[b][:].rearrange("p (a i q) -> p a i q", i=PACK, q=P),
+                raw[:].rearrange("p a c -> p (a c)").bitcast(U16).rearrange("p (a q i) -> p a i q", i=PACK, q=P),
+            )
+
         def load_table_words(a, slot):
             words = keep.tile([P, T], I32, name=slot)
             nc.sync.dma_start(words[:], tab_words[a].rearrange("p t i -> p (t i)").bitcast(I32))
@@ -96,14 +105,14 @@ def tile_list_waggle_patch_scores_kernel(
         def grouped_tile(columns):
             return ring.tile([P, columns * PACK], BF16, name="grouped", bufs=3, align_bytes=64)
 
-        def steps(src, dst, grouped, words, scales):
+        def steps(copy, src, dst, grouped, words, scales):
             half = src.shape[1] // 2
 
             def first():
-                nc.scalar.copy(dst[:, 0:half], src[:, 0:half])
+                copy(dst[:, 0:half], src[:, 0:half])
 
             def second():
-                nc.scalar.copy(dst[:, half : 2 * half], src[:, half : 2 * half])
+                copy(dst[:, half : 2 * half], src[:, half : 2 * half])
                 nc.vector.quantize_mx(out=words.bitcast(FP8X4), scales=scales, in_=grouped[:])
 
             return [first, second]
@@ -112,19 +121,19 @@ def tile_list_waggle_patch_scores_kernel(
             grouped = grouped_tile(PASS)
             dst = grouped[:].rearrange("p (i q j) -> p q i j", i=PACK, j=PACK)
             src = raw[:].rearrange("p j (q i) -> p q i j", i=PACK)
-            return steps(src, dst, grouped, w2_w[b][a][:], w2_s[b][a][:])
+            return steps(nc.scalar.copy, src, dst, grouped, w2_w[b][a][:], w2_s[b][a][:])
 
         def w3_steps(raw, b, c):
             grouped = grouped_tile(W3_PIECE)
             dst = grouped[:].rearrange("p (c i j) -> p c j i", i=4, j=PACK)
             src = raw[:].rearrange("p j (c i) -> p c j i", i=4)
-            return steps(src, dst, grouped, w3_w[b][c][:], w3_s[b][c][:])
+            return steps(nc.scalar.copy, src, dst, grouped, w3_w[b][c][:], w3_s[b][c][:])
 
         def z_steps(b, m0, m1):
             grouped = grouped_tile(m1 - m0)
             dst = grouped[:].rearrange("p (c i j) -> p c j i", i=4, j=PACK)
-            src = z_planes[(b, m0)][:].rearrange("p j (c i) -> p c j i", i=4)
-            return steps(src, dst, grouped, z_w[b][:, m0:m1], z_s[b][:, m0:m1])
+            src = z_planes[b][:, :, m0:m1].rearrange("p j (c i) -> p c j i", i=4)
+            return steps(nc.scalar.copy, src, dst, grouped, z_w[b][:, m0:m1], z_s[b][:, m0:m1])
 
         nc.sync.dma_start(idx[:], offs)
         nc.sync.dma_start(idx_a[:], offs2)
@@ -132,9 +141,7 @@ def tile_list_waggle_patch_scores_kernel(
         nc.gpsimd.dma_start(bias[:], b2.rearrange("(b p i) -> p b i", p=P, i=PACK))
         load_scale_rows(w1_raw_s, w1_scales)
         load_scale_rows(tab_s, tab_scales)
-        nc.sync.dma_start(
-            w1_raw[:].rearrange("p (a c) -> p a c", a=PASSES), w1_words.bitcast(I32).rearrange("a p c -> p a c")
-        )
+        w1_first = load_w1_words(0, "w1_first")
         tab_first = load_table_words(0, "slot_b")
         w2_first = load_rows(w2, 0, slice(0, PASS), "slot_a")
         tab_second = load_table_words(1, "slot_c")
@@ -146,10 +153,7 @@ def tile_list_waggle_patch_scores_kernel(
         move_scale_rows(nc.gpsimd, w1_s, w1_dealt_s)
         nc.vector.tensor_copy(picked_s[:], tab_s[:].indirect(idx[:]))
         move_scale_rows(nc.scalar, v_planes, picked_s)
-        nc.vector.tensor_copy(
-            w1_w[:].rearrange("p (g i q) -> p g i q", i=PACK, q=P),
-            w1_raw[:].bitcast(U16).rearrange("p (g q i) -> p g i q", i=PACK, q=P),
-        )
+        deal_w1_words(w1_first, 0)
         nc.vector.tensor_copy(v_w[0][:], tab_first[:].bitcast(U32).indirect(idx[:]))
         w2_second = load_rows(w2, 1, slice(0, PASS), "slot_b")
         weights = keep.tile([P, 2, M], F32, name="picked_s")
@@ -174,12 +178,13 @@ def tile_list_waggle_patch_scores_kernel(
         nc.vector.tensor_copy(others[:, 1:3], by_plane[:, 2:4])
         nc.vector.quantize_mx(out=w2_w[0][1][:, P:PASS].bitcast(FP8X4), scales=w2_s[0][1][:, P:PASS], in_=other_planes[:])
 
+        deal_w1_words(load_w1_words(1, "w1_dealt_s"), 1)
         w2_late = [load_rows(w2, a, slice(PASS, 2 * PASS), ("slot_a", "slot_c")[a]) for a in range(PASSES)]
 
         def load_w3(b, c):
             return load_rows(w3, b, slice(c * W3_PIECE, (c + 1) * W3_PIECE), ("slot_b", "slot_a")[c])
 
-        def make_h(b, i, slot):
+        def make_h(b, i, shared):
             halves = [slice(c * BANK, (c + 1) * BANK) for c in range(2)]
             angle = [psum.tile([P, BANK], F32, name="angle") for c in range(2)]
             length = [psum.tile([P, BANK], F32, name="length") for c in range(2)]
@@ -199,14 +204,18 @@ def tile_list_waggle_patch_scores_kernel(
                     col = a * H + b * PASS + i * P
                     nc.tensor.matmul_mx(
                         out=length[c][:],
-                        lhsT=w1_w[:, col : col + P].bitcast(FP4X4),
+                        lhsT=w1_w[b][:, a * PASS + i * P : a * PASS + (i + 1) * P].bitcast(FP4X4),
                         lhsT_scale=w1_s[:, col : col + P],
                         rhs=v_w[a][:, halves[c]].bitcast(FP8X4),
                         rhs_scale=v_s[a][:, halves[c]],
                         start=(a == 0),
                         stop=(a == PASSES - 1),
                     )
-            size = [ring.tile([P, BANK], F32, name="size", bufs=2), keep.tile([P, BANK], F32, name=slot)]
+            size = [ring.tile([P, BANK], F32, name="size", bufs=3)]
+            if shared:
+                size.append(keep.tile([P, BANK], F32, name="late_picks"))
+            else:
+                size.append(ring.tile([P, BANK], F32, name="size", bufs=3))
             cosine = [ring.tile([P, BANK], F32, name="cosine", bufs=4) for c in range(2)]
             for c in range(2):
                 nc.scalar.activation(size[c][:], angle[c][:], ACT.Abs, bias=bias[:, b, i : i + 1])
@@ -219,9 +228,6 @@ def tile_list_waggle_patch_scores_kernel(
 
         def pick(x, h, lists, weight, m0, m1):
             nc.vector.tensor_tensor(x, h[:].indirect(lists[:, m0 // LIST_COLS : m1 // LIST_COLS]), weight[:, m0:m1], ALU.mult)
-
-        def z_part(b, i, m0, m1):
-            return z_planes[(0, 0)][:, i, m0:m1] if b == 0 else z_planes[(1, m0)][:, i, :]
 
         def score_passes(y, b, n0, m0, m1):
             per_bank = BANK // (m1 - m0)
@@ -254,37 +260,37 @@ def tile_list_waggle_patch_scores_kernel(
             lambda: w3_steps(w3_raw[1][0], 1, 0),
             lambda: w3_steps(w3_raw[1][1], 1, 1),
         ]
-        side_counts = (1, 2, 1, 2, 2, 1, 2, 3)
+        side_counts = (0, 2, 2, 2, 2, 1, 2, 3)
         pending = []
         made = 0
         tiles = [(b, i) for b in range(BLOCKS) for i in range(PACK)]
         low, high = M_CHUNKS
         last = len(tiles) - 1
-        before = None
+        lo, hi = slice(*low), slice(*high)
         for t, (b, i) in enumerate(tiles):
-            slot = "size_high%d" % (t % 2)
-            h = make_h(b, i, slot)
+            h = make_h(b, i, t == last)
             xa = ring.tile([P, M], F32, name="xa", bufs=3)
-            xb_low = ring.tile([P, low[1]], F32, name="xb", bufs=3)
-            if before is not None:
-                xb_high = keep.tile([P, M - low[1]], F32, name=slot)
-                pick(xb_high[:], before[0], idx_b, wb, *high)
-            if t < last:
+            xb = ring.tile([P, M], F32, name="xb", bufs=3)
+            if t < last - 1:
                 pick(xa[:], h, idx_a, wa, 0, M)
+                pick(xb[:], h, idx_b, wb, 0, M)
+                nc.gpsimd.tensor_tensor(z_planes[b][:, i, :], xa[:], xb[:], ALU.add)
+            elif t < last:
+                pick(xa[:, lo], h, idx_a, wa, *low)
+                pick(xb[:, lo], h, idx_b, wb, *low)
+                nc.gpsimd.tensor_tensor(z_planes[b][:, i, lo], xa[:, lo], xb[:, lo], ALU.add)
+                h_before = h
             else:
-                pick(xa[:, 0 : low[1]], h, idx_a, wa, *low)
-            if before is not None:
-                nc.vector.tensor_tensor(z_part(*tiles[t - 1], *high), before[1][:, low[1] : M], xb_high[:], ALU.add)
-            pick(xb_low[:], h, idx_b, wb, *low)
-            if t < last:
-                nc.gpsimd.tensor_tensor(z_part(b, i, *low), xa[:, 0 : low[1]], xb_low[:], ALU.add)
-            else:
-                xb_high = ring.tile([P, M - low[1]], F32, name="xb", bufs=3)
-                pick(xa[:, low[1] : M], h, idx_a, wa, *high)
-                nc.vector.tensor_tensor(z_part(b, i, *low), xa[:, 0 : low[1]], xb_low[:], ALU.add)
-                pick(xb_high[:], h, idx_b, wb, *high)
-                nc.vector.tensor_tensor(z_part(b, i, *high), xa[:, low[1] : M], xb_high[:], ALU.add)
-            before = (h, xa)
+                late = keep.tile([P, 2, high[1] - high[0]], F32, name="late_picks")
+                pick(late[:, 0, :], h_before, idx_a, wa, *high)
+                pick(xa[:, lo], h, idx_a, wa, *low)
+                pick(xb[:, lo], h, idx_b, wb, *low)
+                nc.vector.tensor_tensor(z_planes[b][:, i, lo], xa[:, lo], xb[:, lo], ALU.add)
+                pick(late[:, 1, :], h_before, idx_b, wb, *high)
+                nc.vector.tensor_tensor(z_planes[b][:, i - 1, hi], late[:, 0, :], late[:, 1, :], ALU.add)
+                pick(xa[:, hi], h, idx_a, wa, *high)
+                pick(xb[:, hi], h, idx_b, wb, *high)
+                nc.vector.tensor_tensor(z_planes[b][:, i, hi], xa[:, hi], xb[:, hi], ALU.add)
             for u in range(side_counts[t]):
                 if not pending:
                     pending = side_makers[made]()

import math
from contextlib import ExitStack

import concourse.mybir as mybir

K, H, N, T, S, M = 1024, 1024, 768, 4096, 1024, 512
FLOPS = 2 * (2 * K * H * S + H * N * M)

F32 = mybir.dt.float32
BF16 = mybir.dt.bfloat16
I32 = mybir.dt.int32
U32 = mybir.dt.uint32
U16 = mybir.dt.uint16
U8 = mybir.dt.uint8
FP8X4 = mybir.dt.float8_e4m3fn_x4
FP4X4 = mybir.dt.float4_e2m1fn_x4
ALU = mybir.AluOpType
ACT = mybir.ActivationFunctionType

P = 128
PACK = 4
PASS = P * PACK
BANK = 512
PASSES = K // PASS
BLOCKS = H // PASS
N_TILES = N // P
W3_PIECE = N // 2
LIST_COLS = 16
M_CHUNKS = ((0, 256), (256, 512))


def tile_list_waggle_patch_scores_kernel(
    tc, tab_words, tab_scales, w1_words, w1_scales, w2, b2, w3, wga, wgb, land, offs, offs2, offs3, out
):
    nc = tc.nc
    with ExitStack() as ctx:
        keep = ctx.enter_context(tc.tile_pool(name="keep", bufs=1))
        ring = ctx.enter_context(tc.tile_pool(name="ring", bufs=2))
        psum = ctx.enter_context(tc.psum_pool(name="psum", bufs=2))

        idx = keep.tile([P, S // LIST_COLS], U16, name="idx")
        idx_a = keep.tile([P, M // LIST_COLS], U16, name="idx_a")
        idx_b = keep.tile([P, M // LIST_COLS], U16, name="idx_b")
        bias = keep.tile([P, BLOCKS, PACK], F32, name="bias")
        half_pi = keep.tile([P, 1], F32, name="half_pi")
        one = keep.tile([P, 1], F32, name="one")
        warm = keep.tile([P, 1], F32, name="warm")
        tab_s = keep.tile([P, T], U8, name="tab_s")
        picked_s = keep.tile([P, S], U8, name="picked_s")
        w1_raw_s = keep.tile([P, H], U8, name="w1_raw_s")
        w1_dealt_s = keep.tile([P, H], U8, name="w1_dealt_s")
        w1_w = [keep.tile([P, PASSES * PASS], U16, name="w1_w%d" % b, align_bytes=64) for b in range(BLOCKS)]
        w1_s = keep.tile([P, PASSES * H], U8, name="w1_s", align_bytes=64)
        v_w = [keep.tile([P, S], U32, name="v_w%d" % a, align_bytes=64) for a in range(PASSES)]
        v_planes = keep.tile([P, PASSES * S], U8, name="v_planes", align_bytes=64)
        v_s = [v_planes[:, a * S : (a + 1) * S] for a in range(PASSES)]
        w2_w = [[keep.tile([P, PASS], U32, name="w2_w%d%d" % (b, a), align_bytes=64) for a in range(PASSES)] for b in range(BLOCKS)]
        w2_s = [[keep.tile([P, PASS], U8, name="w2_s%d%d" % (b, a), align_bytes=64) for a in range(PASSES)] for b in range(BLOCKS)]
        w3_w = [[keep.tile([P, W3_PIECE], U32, name="w3_w%d%d" % (b, c), align_bytes=64) for c in range(2)] for b in range(BLOCKS)]
        w3_s = [[keep.tile([P, W3_PIECE], U8, name="w3_s%d%d" % (b, c), align_bytes=64) for c in range(2)] for b in range(BLOCKS)]
        z_planes = [keep.tile([P, PACK, M], BF16, name="z_planes%d" % b) for b in range(BLOCKS)]
        z_w = [keep.tile([P, M], U32, name="z_w%d" % b, align_bytes=64) for b in range(BLOCKS)]
        z_s = [keep.tile([P, M], U8, name="z_s%d" % b, align_bytes=64) for b in range(BLOCKS)]

        nc.vector.memset(tab_s[0:96, :].bitcast(I32), 0)
        nc.vector.memset(w1_raw_s[0:96, :].bitcast(I32), 0)
        nc.gpsimd.memset(w1_s[:].bitcast(I32), 0)
        nc.gpsimd.memset(v_planes[:].bitcast(I32), 0)
        nc.gpsimd.memset(one[:], 1.0)
        nc.gpsimd.tensor_scalar(half_pi[:], one[:], math.pi / 2, 0.0, ALU.mult, ALU.add)
        nc.scalar.activation(warm[:], one[:], ACT.Sin)

        def load_scale_rows(rows, scales):
            nc.sync.dma_start(rows[96:P, :].bitcast(I32), scales.bitcast(I32).rearrange("a q t -> q a t"))

        def move_scale_rows(queue, planes, rows):
            for q in range(4):
                queue.dma_start(
                    planes[32 * q : 32 * q + 4, :].bitcast(I32).rearrange("p (a t) -> p a t", a=PASSES),
                    rows[96 + 8 * q : 96 + 8 * q + 8, :].bitcast(I32),
                )

        def load_w1_words(b, slot):
            raw = keep.tile([P, PASSES, PASS // 2], I32, name=slot)
            rows = w1_words.bitcast(I32).rearrange("a p c -> p a c")
            nc.sync.dma_start(raw[:], rows[:, :, b * PASS // 2 : (b + 1) * PASS // 2])
            return raw

        def deal_w1_words(raw, b):
            nc.vector.tensor_copy(
                w1_w[b][:].rearrange("p (a i q) -> p a i q", i=PACK, q=P),
                raw[:].rearrange("p a c -> p (a c)").bitcast(U16).rearrange("p (a q i) -> p a i q", i=PACK, q=P),
            )

        def load_table_words(a, slot):
            words = keep.tile([P, T], I32, name=slot)
            nc.sync.dma_start(words[:], tab_words[a].rearrange("p t i -> p (t i)").bitcast(I32))
            return words

        def load_rows(w, a, cols, slot):
            raw = keep.tile([P, PACK, cols.stop - cols.start], F32, name=slot)
            nc.sync.dma_start(raw[:], w[a * PASS : (a + 1) * PASS, cols].rearrange("(p j) c -> p j c", j=PACK))
            return raw

        def grouped_tile(columns):
            return ring.tile([P, columns * PACK], BF16, name="grouped", bufs=3, align_bytes=64)

        def steps(copy, src, dst, grouped, words, scales):
            half = src.shape[1] // 2

            def first():
                copy(dst[:, 0:half], src[:, 0:half])

            def second():
                copy(dst[:, half : 2 * half], src[:, half : 2 * half])
                nc.vector.quantize_mx(out=words.bitcast(FP8X4), scales=scales, in_=grouped[:])

            return [first, second]

        def w2_steps(raw, b, a):
            grouped = grouped_tile(PASS)
            dst = grouped[:].rearrange("p (i q j) -> p q i j", i=PACK, j=PACK)
            src = raw[:].rearrange("p j (q i) -> p q i j", i=PACK)
            return steps(nc.scalar.copy, src, dst, grouped, w2_w[b][a][:], w2_s[b][a][:])

        def w3_steps(raw, b, c):
            grouped = grouped_tile(W3_PIECE)
            dst = grouped[:].rearrange("p (c i j) -> p c j i", i=4, j=PACK)
            src = raw[:].rearrange("p j (c i) -> p c j i", i=4)
            return steps(nc.scalar.copy, src, dst, grouped, w3_w[b][c][:], w3_s[b][c][:])

        def z_steps(b, m0, m1):
            grouped = grouped_tile(m1 - m0)
            dst = grouped[:].rearrange("p (c i j) -> p c j i", i=4, j=PACK)
            src = z_planes[b][:, :, m0:m1].rearrange("p j (c i) -> p c j i", i=4)
            return steps(nc.scalar.copy, src, dst, grouped, z_w[b][:, m0:m1], z_s[b][:, m0:m1])

        nc.sync.dma_start(idx[:], offs)
        nc.sync.dma_start(idx_a[:], offs2)
        nc.sync.dma_start(idx_b[:], offs3)
        nc.gpsimd.dma_start(bias[:], b2.rearrange("(b p i) -> p b i", p=P, i=PACK))
        load_scale_rows(w1_raw_s, w1_scales)
        load_scale_rows(tab_s, tab_scales)
        w1_first = load_w1_words(0, "w1_first")
        tab_first = load_table_words(0, "slot_b")
        w2_first = load_rows(w2, 0, slice(0, PASS), "slot_a")
        tab_second = load_table_words(1, "slot_c")

        nc.vector.tensor_copy(
            w1_dealt_s[:].rearrange("p (g i q) -> p g i q", i=PACK, q=P),
            w1_raw_s[:].rearrange("p (g q i) -> p g i q", i=PACK, q=P),
        )
        move_scale_rows(nc.gpsimd, w1_s, w1_dealt_s)
        nc.vector.tensor_copy(picked_s[:], tab_s[:].indirect(idx[:]))
        move_scale_rows(nc.scalar, v_planes, picked_s)
        deal_w1_words(w1_first, 0)
        nc.vector.tensor_copy(v_w[0][:], tab_first[:].bitcast(U32).indirect(idx[:]))
        w2_second = load_rows(w2, 1, slice(0, PASS), "slot_b")
        weights = keep.tile([P, 2, M], F32, name="picked_s")
        wa = weights[:, 0, :]
        wb = weights[:, 1, :]
        nc.sync.dma_start(wa, wga)
        nc.sync.dma_start(wb, wgb)
        for step in w2_steps(w2_first, 0, 0):
            step()
        for c in range(2):
            nc.vector.tensor_copy(
                v_w[1][:, c * BANK : (c + 1) * BANK],
                tab_second[:].bitcast(U32).indirect(idx[:, c * BANK // LIST_COLS : (c + 1) * BANK // LIST_COLS]),
            )
        by_plane = w2_second[:].rearrange("p j (q i) -> p i q j", i=PACK)
        first_plane = grouped_tile(P)
        nc.vector.tensor_copy(first_plane[:].rearrange("p (q j) -> p q j", j=PACK), by_plane[:, 0])
        nc.vector.quantize_mx(out=w2_w[0][1][:, 0:P].bitcast(FP8X4), scales=w2_s[0][1][:, 0:P], in_=first_plane[:])
        other_planes = grouped_tile(PASS - P)
        others = other_planes[:].rearrange("p (i q j) -> p i q j", q=P, j=PACK)
        nc.scalar.copy(others[:, 0], by_plane[:, 1])
        nc.vector.tensor_copy(others[:, 1:3], by_plane[:, 2:4])
        nc.vector.quantize_mx(out=w2_w[0][1][:, P:PASS].bitcast(FP8X4), scales=w2_s[0][1][:, P:PASS], in_=other_planes[:])

        deal_w1_words(load_w1_words(1, "w1_dealt_s"), 1)
        w2_late = [load_rows(w2, a, slice(PASS, 2 * PASS), ("slot_a", "slot_c")[a]) for a in range(PASSES)]

        def load_w3(b, c):
            return load_rows(w3, b, slice(c * W3_PIECE, (c + 1) * W3_PIECE), ("slot_b", "slot_a")[c])

        def make_h(b, i, shared):
            halves = [slice(c * BANK, (c + 1) * BANK) for c in range(2)]
            angle = [psum.tile([P, BANK], F32, name="angle") for c in range(2)]
            length = [psum.tile([P, BANK], F32, name="length") for c in range(2)]
            for c in range(2):
                for a in range(PASSES):
                    nc.tensor.matmul_mx(
                        out=angle[c][:],
                        lhsT=w2_w[b][a][:, i * P : (i + 1) * P].bitcast(FP8X4),
                        lhsT_scale=w2_s[b][a][:, i * P : (i + 1) * P],
                        rhs=v_w[a][:, halves[c]].bitcast(FP8X4),
                        rhs_scale=v_s[a][:, halves[c]],
                        start=(a == 0),
                        stop=(a == PASSES - 1),
                    )
            for c in range(2):
                for a in range(PASSES):
                    col = a * H + b * PASS + i * P
                    nc.tensor.matmul_mx(
                        out=length[c][:],
                        lhsT=w1_w[b][:, a * PASS + i * P : a * PASS + (i + 1) * P].bitcast(FP4X4),
                        lhsT_scale=w1_s[:, col : col + P],
                        rhs=v_w[a][:, halves[c]].bitcast(FP8X4),
                        rhs_scale=v_s[a][:, halves[c]],
                        start=(a == 0),
                        stop=(a == PASSES - 1),
                    )
            size = [ring.tile([P, BANK], F32, name="size", bufs=3)]
            if shared:
                size.append(keep.tile([P, BANK], F32, name="late_picks"))
            else:
                size.append(ring.tile([P, BANK], F32, name="size", bufs=3))
            cosine = [ring.tile([P, BANK], F32, name="cosine", bufs=4) for c in range(2)]
            for c in range(2):
                nc.scalar.activation(size[c][:], angle[c][:], ACT.Abs, bias=bias[:, b, i : i + 1])
            for c in range(2):
                nc.scalar.activation(cosine[c][:], size[c][:], ACT.Sin, bias=half_pi[:], scale=-1.0)
            h = ring.tile([P, S], F32, name="h", bufs=3)
            for c in range(2):
                nc.vector.tensor_tensor(h[:, halves[c]], length[c][:], cosine[c][:], ALU.mult)
            return h

        def pick(x, h, lists, weight, m0, m1):
            nc.vector.tensor_tensor(x, h[:].indirect(lists[:, m0 // LIST_COLS : m1 // LIST_COLS]), weight[:, m0:m1], ALU.mult)

        def score_passes(y, b, n0, m0, m1):
            per_bank = BANK // (m1 - m0)
            for u in range(per_bank):
                c, col = divmod((n0 + u) * P, W3_PIECE)
                nc.tensor.matmul_mx(
                    out=y[:, u, :],
                    lhsT=w3_w[b][c][:, col : col + P].bitcast(FP8X4),
                    lhsT_scale=w3_s[b][c][:, col : col + P],
                    rhs=z_w[b][:, m0:m1].bitcast(FP8X4),
                    rhs_scale=z_s[b][:, m0:m1],
                    start=(b == 0 and u == 0),
                    stop=(b == BLOCKS - 1 and u == per_bank - 1),
                )

        def weigh_and_store(y, n0, m0, m1, u0, u1, queue):
            result = ring.tile([P, u1 - u0, m1 - m0], F32, name="result", bufs=7)
            nc.vector.tensor_tensor(result[:], y[:, u0:u1, :], land_t[:, n0 + u0 : n0 + u1, m0:m1], ALU.mult)
            queue.dma_start(out[(n0 + u0) * P : (n0 + u1) * P, m0:m1].rearrange("(t p) m -> p t m", p=P), result[:])

        w3_raw = [[load_w3(b, c) for c in range(2)] for b in range(BLOCKS)]
        land_t = keep.tile([P, N_TILES, M], F32, name="slot_c")
        nc.sync.dma_start(land_t[:], land.rearrange("(t p) m -> p t m", p=P))
        side_makers = [
            lambda: w2_steps(w2_late[0], 1, 0),
            lambda: w2_steps(w2_late[1], 1, 1),
            lambda: w3_steps(w3_raw[0][0], 0, 0),
            lambda: w3_steps(w3_raw[0][1], 0, 1),
            lambda: z_steps(0, 0, M),
            lambda: w3_steps(w3_raw[1][0], 1, 0),
            lambda: w3_steps(w3_raw[1][1], 1, 1),
        ]
        side_counts = (0, 2, 2, 2, 2, 1, 2, 3)
        pending = []
        made = 0
        tiles = [(b, i) for b in range(BLOCKS) for i in range(PACK)]
        low, high = M_CHUNKS
        last = len(tiles) - 1
        lo, hi = slice(*low), slice(*high)
        for t, (b, i) in enumerate(tiles):
            h = make_h(b, i, t == last)
            xa = ring.tile([P, M], F32, name="xa", bufs=3)
            xb = ring.tile([P, M], F32, name="xb", bufs=3)
            if t < last - 1:
                pick(xa[:], h, idx_a, wa, 0, M)
                pick(xb[:], h, idx_b, wb, 0, M)
                nc.gpsimd.tensor_tensor(z_planes[b][:, i, :], xa[:], xb[:], ALU.add)
            elif t < last:
                pick(xa[:, lo], h, idx_a, wa, *low)
                pick(xb[:, lo], h, idx_b, wb, *low)
                nc.gpsimd.tensor_tensor(z_planes[b][:, i, lo], xa[:, lo], xb[:, lo], ALU.add)
                h_before = h
            else:
                late = keep.tile([P, 2, high[1] - high[0]], F32, name="late_picks")
                pick(late[:, 0, :], h_before, idx_a, wa, *high)
                pick(xa[:, lo], h, idx_a, wa, *low)
                pick(xb[:, lo], h, idx_b, wb, *low)
                nc.vector.tensor_tensor(z_planes[b][:, i, lo], xa[:, lo], xb[:, lo], ALU.add)
                pick(late[:, 1, :], h_before, idx_b, wb, *high)
                nc.vector.tensor_tensor(z_planes[b][:, i - 1, hi], late[:, 0, :], late[:, 1, :], ALU.add)
                pick(xa[:, hi], h, idx_a, wa, *high)
                pick(xb[:, hi], h, idx_b, wb, *high)
                nc.vector.tensor_tensor(z_planes[b][:, i, hi], xa[:, hi], xb[:, hi], ALU.add)
            for u in range(side_counts[t]):
                if not pending:
                    pending = side_makers[made]()
                    made = made + 1
                pending[0]()
                pending = pending[1:]

        banks = []
        for m0, m1 in M_CHUNKS:
            for n0 in range(0, N_TILES, BANK // (m1 - m0)):
                if len(banks) < 4:
                    y = psum.tile([P, BANK // (m1 - m0), m1 - m0], F32, name="scores", bufs=4)
                else:
                    y = psum.tile([P, BANK // (m1 - m0), m1 - m0], F32, name="angle")
                banks.append((y, n0, m0, m1))
                score_passes(y, 0, n0, m0, m1)
        for m0, m1 in M_CHUNKS:
            for step in z_steps(1, m0, m1):
                step()
        for y, n0, m0, m1 in banks:
            score_passes(y, 1, n0, m0, m1)
            if y is banks[-1][0]:
                weigh_and_store(y, n0, m0, m1, 0, 1, nc.sync)
                weigh_and_store(y, n0, m0, m1, 1, 2, nc.scalar)
            else:
                weigh_and_store(y, n0, m0, m1, 0, 2, nc.sync)
